import numpy as np
import ml_dtypes


def mxq(x, axis, fmt="e4m3"):
    dtype, down = {"e4m3": (ml_dtypes.float8_e4m3fn, 7), "e5m2": (ml_dtypes.float8_e5m2, 14)}[fmt]
    v = np.moveaxis(np.asarray(x, np.float32).astype(ml_dtypes.bfloat16).astype(np.float64), axis, -1)
    blocks = v.reshape(v.shape[:-1] + (-1, 32))
    amax = np.abs(blocks).max(-1, keepdims=True)
    byte = np.maximum(np.where(amax > 0, np.frexp(amax)[1] - 1 + 127, 0) - down, 1)
    scale = np.exp2(byte - 127.0)
    codes = (blocks / scale).astype(np.float32).astype(dtype).astype(np.float64)
    return np.moveaxis((codes * scale).reshape(v.shape), -1, axis)


WIDE = False


def mx_kscale(k):
    if not WIDE:
        return np.ones(k)
    levels = np.array([10, -10, 5, -5, 0])
    if k % 512:
        return np.exp2(np.random.permutation(np.resize(levels, k // 32))).repeat(32)
    a = np.empty((k // 512, 16))
    for p in range(k // 512):
        a[p, :8] = np.random.permutation(np.resize(levels, 8))
        for g in range(8):
            far = levels[np.abs(levels - a[p, g]) >= 10]
            a[p, g + 8] = far[np.random.randint(len(far))]
    return np.exp2(a.ravel()).repeat(32)


def f64(x):
    return np.asarray(x).astype(np.float64)


def striped(idx):
    return np.tile(idx.reshape(-1, 16).T, (8, 1)).astype(np.uint16)


def unstriped(offs):
    return offs[:16].T.reshape(-1).astype(np.int64)


def pack_weight(w):
    k, n = w.shape
    w = f64(np.asarray(w, np.float32).astype(ml_dtypes.bfloat16)).reshape(k // 32, 32, n)
    amax = np.abs(w).max(1)
    byte = np.clip(np.where(amax > 0, np.frexp(amax)[1] - 1 + 127 - 7, 1), 1, 254)
    scaled = (w * np.exp2(127.0 - byte)[:, None, :]).reshape(k, n).astype(np.float32)
    words = np.ascontiguousarray(scaled.reshape(k // 512, 128, 4, n).transpose(0, 1, 3, 2)).astype(ml_dtypes.float8_e4m3fn).view(np.uint8)
    return words, np.ascontiguousarray(byte.astype(np.uint8).reshape(k // 512, 16, n))


def unpack_weight(words, scales):
    g, p, n, _ = words.shape
    vals = np.ascontiguousarray(words).view(ml_dtypes.float8_e4m3fn).astype(np.float64) * np.repeat(np.exp2(scales.astype(np.float64) - 127.0), 8, axis=1)[..., None]
    return vals.transpose(0, 1, 3, 2).reshape(g * 512, n)


def sigmoid(v):
    return 1.0 / (1.0 + np.exp(-np.maximum(v, -700.0)))


K, T, S, V = 1024, 1024, 512, 256


def setup_inputs():
    n = np.random.standard_normal
    s = mx_kscale(K)[:, None]
    packed_xT = pack_weight(n((K, T)) * s)
    return {
        "x_words": packed_xT[0],
        "x_scales": packed_xT[1],
        "hT": (n((K, V)) / np.sqrt(K) / s).astype(np.float32),
        "offs": striped(np.random.permutation(T)[:S]),
    }


def reference(x_words, x_scales, hT, offs):
    hTq = mxq(f64(hT), 0, "e4m3")
    xq = unpack_weight(x_words, x_scales)[:, unstriped(offs)]
    y = hTq.T @ xq
    ex = np.exp(y - y.max(axis=1, keepdims=True))
    pr = 100.0 * (ex / ex.sum(axis=1, keepdims=True))
    sm = (np.pad(pr, ((0, 0), (1, 0)))[:, :S] + pr + np.pad(pr, ((0, 0), (0, 1)))[:, 1:]) / 3
    mean = sm.mean(axis=1, keepdims=True)
    return pr * (sigmoid(4.0 * (sm - (1.5 * mean)))) + 0.2 * sm

@@ -1,0 +1,139 @@
+from contextlib import ExitStack
+
+import concourse.mybir as mybir
+
+K, T, S, V = 1024, 1024, 512, 256
+FLOPS = 2 * K * S * V
+
+F32 = mybir.dt.float32
+BF16 = mybir.dt.bfloat16
+I32 = mybir.dt.int32
+U32 = mybir.dt.uint32
+U16 = mybir.dt.uint16
+U8 = mybir.dt.uint8
+FP8X4 = mybir.dt.float8_e4m3fn_x4
+ALU = mybir.AluOpType
+ACT = mybir.ActivationFunctionType
+AX = mybir.AxisListType
+
+P = 128
+PACK = 4
+PASSES = K // (P * PACK)
+TILES = V // P
+PAD = 4
+
+
+def tile_picked_ysnapv_avg_p_kernel(tc, x_words, x_scales, hT, offs, out):
+    nc = tc.nc
+    with ExitStack() as ctx:
+        keep = ctx.enter_context(tc.tile_pool(name="keep", bufs=1))
+        psum = ctx.enter_context(tc.psum_pool(name="psum", bufs=1))
+
+        offsets = keep.tile([P, S // 16], U16, name="offsets")
+        nc.sync.dma_start(offsets[:], offs)
+
+        scale_table = keep.tile([P, T], U8, name="scale_table", align_bytes=64)
+        nc.gpsimd.memset(scale_table[:].bitcast(I32), 0)
+        word_table = [keep.tile([P, T], I32, name="word_table%d" % g, align_bytes=64) for g in range(PASSES)]
+        h_raw = [keep.tile([P, PACK, V], F32, name="h_raw%d" % g, align_bytes=64) for g in range(PASSES)]
+
+        def load_words(g):
+            nc.sync.dma_start(word_table[g][:], x_words[g].rearrange("p n t -> p (n t)").bitcast(I32))
+
+        def load_h(g):
+            nc.sync.dma_start(h_raw[g][:], hT[512 * g : 512 * (g + 1), :].rearrange("(p j) v -> p j v", j=PACK))
+
+        load_words(0)
+        for q in range(4):
+            nc.sync.dma_start(
+                scale_table[32 * q : 32 * q + 4 * PASSES, :].bitcast(I32),
+                x_scales[:, 4 * q : 4 * q + 4, :].bitcast(I32),
+            )
+        load_h(0)
+        load_words(1)
+        load_h(1)
+
+        zero = keep.tile([P, 2], F32, name="zero")
+        nc.gpsimd.memset(zero[:], 0.0)
+        ex = [keep.tile([P, S + 2 * PAD], F32, name="ex%d" % m, align_bytes=64) for m in range(TILES)]
+        for m in range(TILES):
+            nc.scalar.activation(ex[m][:, PAD - 1 : PAD + S + 1 : S + 1], zero[:], ACT.Copy)
+        numer = keep.tile([P, 4], F32, name="numer")
+        for col, value in enumerate((200.0, 150.0, 20.0, 300.0 / S)):
+            nc.gpsimd.memset(numer[:, col : col + 1], value)
+        factors = keep.tile([P, 4], F32, name="factors")
+        nc.gpsimd.tensor_scalar(factors[:], numer[:], 1.0 / 3.0, 0.0, ALU.mult, ALU.add)
+
+        key_scales = keep.tile([P, S], U8, name="key_scales", align_bytes=64)
+        key_words = [keep.tile([P, S], U32, name="key_words%d" % g, align_bytes=64) for g in range(PASSES)]
+
+        def gather_words(g):
+            nc.vector.tensor_copy(key_words[g][:], word_table[g][:].bitcast(U32).indirect(offsets[:]))
+
+        gather_words(0)
+        nc.vector.tensor_copy(key_scales[:], scale_table[:].indirect(offsets[:]))
+
+        h_bf, h_words, h_scales = {}, {}, {}
+        for g in range(PASSES):
+            for m in range(TILES):
+                h_bf[g, m] = keep.tile([P, P * PACK], BF16, name="h_bf%d%d" % (g, m), align_bytes=64)
+                h_words[g, m] = keep.tile([P, P], U32, name="h_words%d%d" % (g, m), align_bytes=64)
+                h_scales[g, m] = keep.tile([P, P], U8, name="h_scales%d%d" % (g, m), align_bytes=64)
+
+        def weave(g, m, on_vector):
+            dst = h_bf[g, m][:].rearrange("p (c i t) -> p c t i", i=4, t=PACK)
+            src = h_raw[g][:, :, P * m : P * (m + 1)].rearrange("p t (c i) -> p c t i", i=4)
+            if on_vector:
+                nc.vector.tensor_copy(dst, src)
+            else:
+                nc.scalar.activation(dst, src, ACT.Copy)
+
+        scores = [psum.tile([P, S], F32, name="scores%d" % m) for m in range(TILES)]
+
+        def quantise_and_multiply(g, m):
+            nc.vector.quantize_mx(out=h_words[g, m][:].bitcast(FP8X4), scales=h_scales[g, m][:], in_=h_bf[g, m][:])
+            nc.tensor.matmul_mx(
+                out=scores[m][:],
+                lhsT=h_words[g, m][:].bitcast(FP8X4),
+                lhsT_scale=h_scales[g, m][:],
+                rhs=key_words[g][:].bitcast(FP8X4),
+                rhs_scale=key_scales[4 * g : P, :],
+                start=(g == 0),
+                stop=(g == PASSES - 1),
+            )
+
+        weave(0, 0, False)
+        weave(0, 1, True)
+        quantise_and_multiply(0, 0)
+        quantise_and_multiply(0, 1)
+        gather_words(1)
+        weave(1, 0, False)
+        weave(1, 1, True)
+        quantise_and_multiply(1, 0)
+        quantise_and_multiply(1, 1)
+
+        def small(name, cols=1):
+            return [keep.tile([P, cols], F32, name="%s%d" % (name, m)) for m in range(TILES)]
+
+        def wide(name):
+            return [keep.tile([P, S], F32, name="%s%d" % (name, m), align_bytes=64) for m in range(TILES)]
+
+        neg_max, total, inv, ends, coef, shift = small("neg_max"), small("total"), small("inv"), small("ends"), small("coef", 4), small("shift")
+        sides, three, half_pr, th, gated, result = wide("sides"), wide("three"), wide("half_pr"), wide("th"), wide("gated"), wide("result")
+
+        for m in range(TILES):
+            nc.vector.tensor_reduce(neg_max[m][:], scores[m][:], AX.X, ALU.max, negate=True)
+            nc.scalar.activation(ex[m][:, PAD : PAD + S], scores[m][:], ACT.Exp, bias=neg_max[m][:], accum_out=total[m][:])
+        for m in range(TILES):
+            nc.vector.reciprocal(inv[m][:], total[m][:])
+            nc.vector.tensor_tensor(sides[m][:], ex[m][:, PAD - 1 : PAD - 1 + S], ex[m][:, PAD + 1 : PAD + 1 + S], ALU.add)
+            nc.vector.tensor_tensor(three[m][:], sides[m][:], ex[m][:, PAD : PAD + S], ALU.add)
+            nc.scalar.activation(ends[m][:], ex[m][:, PAD : PAD + 1], ACT.Identity, bias=ex[m][:, PAD + S - 1 : PAD + S])
+            nc.scalar.activation(coef[m][:], factors[:], ACT.Copy, scale=inv[m][:])
+            nc.scalar.activation(shift[m][:], ends[m][:], ACT.Copy, scale=coef[m][:, 3:4], bias=-300.0 / S)
+            nc.scalar.activation(half_pr[m][:], ex[m][:, PAD : PAD + S], ACT.Copy, scale=coef[m][:, 1:2])
+            nc.scalar.activation(th[m][:], three[m][:], ACT.Tanh, scale=coef[m][:, 0:1], bias=shift[m][:])
+        for m in range(TILES):
+            nc.vector.scalar_tensor_tensor(gated[m][:], th[m][:], 1.0, half_pr[m][:], ALU.add, ALU.mult)
+            nc.vector.scalar_tensor_tensor(result[m][:], three[m][:], coef[m][:, 2:3], gated[m][:], ALU.mult, ALU.add)
+            nc.sync.dma_start(out[P * m : P * (m + 1), :], result[m][:])

@@ -20,7 +20,12 @@ P = 128
 PACK = 4
 PASSES = K // (P * PACK)
 TILES = V // P
-PAD = 4
+HALF = S // 2
+EVEN = 4
+ROW = HALF + 4
+ODD = EVEN + ROW
+EX_COLS = 528
+LEAD = 4
 
 
 def tile_picked_ysnapv_avg_p_kernel(tc, x_words, x_scales, hT, offs, out):
@@ -30,7 +35,6 @@ def tile_picked_ysnapv_avg_p_kernel(tc, x_words, x_scales, hT, offs, out):
         psum = ctx.enter_context(tc.psum_pool(name="psum", bufs=1))
 
         offsets = keep.tile([P, S // 16], U16, name="offsets")
-        nc.sync.dma_start(offsets[:], offs)
 
         scale_table = keep.tile([P, T], U8, name="scale_table", align_bytes=64)
         nc.gpsimd.memset(scale_table[:].bitcast(I32), 0)
@@ -44,6 +48,7 @@ def tile_picked_ysnapv_avg_p_kernel(tc, x_words, x_scales, hT, offs, out):
             nc.sync.dma_start(h_raw[g][:], hT[512 * g : 512 * (g + 1), :].rearrange("(p j) v -> p j v", j=PACK))
 
         load_words(0)
+        nc.sync.dma_start(offsets[:], offs)
         for q in range(4):
             nc.sync.dma_start(
                 scale_table[32 * q : 32 * q + 4 * PASSES, :].bitcast(I32),
@@ -53,11 +58,12 @@ def tile_picked_ysnapv_avg_p_kernel(tc, x_words, x_scales, hT, offs, out):
         load_words(1)
         load_h(1)
 
-        zero = keep.tile([P, 2], F32, name="zero")
+        zero = keep.tile([P, 2, 2], F32, name="zero")
         nc.gpsimd.memset(zero[:], 0.0)
-        ex = [keep.tile([P, S + 2 * PAD], F32, name="ex%d" % m, align_bytes=64) for m in range(TILES)]
+        ex = [keep.tile([P, EX_COLS], F32, name="ex%d" % m, align_bytes=64) for m in range(TILES)]
         for m in range(TILES):
-            nc.scalar.activation(ex[m][:, PAD - 1 : PAD + S + 1 : S + 1], zero[:], ACT.Copy)
+            borders = ex[m][:, EVEN - 1 : EVEN - 1 + 2 * ROW].rearrange("p (c i) -> p c i", c=2)[:, :, 0 : HALF + 2 : HALF + 1]
+            nc.scalar.activation(borders, zero[:], ACT.Copy)
         numer = keep.tile([P, 4], F32, name="numer")
         for col, value in enumerate((200.0, 150.0, 20.0, 300.0 / S)):
             nc.gpsimd.memset(numer[:, col : col + 1], value)
@@ -65,52 +71,44 @@ def tile_picked_ysnapv_avg_p_kernel(tc, x_words, x_scales, hT, offs, out):
         nc.gpsimd.tensor_scalar(factors[:], numer[:], 1.0 / 3.0, 0.0, ALU.mult, ALU.add)
 
         key_scales = keep.tile([P, S], U8, name="key_scales", align_bytes=64)
-        key_words = [keep.tile([P, S], U32, name="key_words%d" % g, align_bytes=64) for g in range(PASSES)]
+        key_words = {}
 
         def gather_words(g):
+            key_words[g] = keep.tile([P, S], U32, name="key_words%d" % g, tag="stage%d" % g, align_bytes=64)
             nc.vector.tensor_copy(key_words[g][:], word_table[g][:].bitcast(U32).indirect(offsets[:]))
 
         gather_words(0)
         nc.vector.tensor_copy(key_scales[:], scale_table[:].indirect(offsets[:]))
 
-        h_bf, h_words, h_scales = {}, {}, {}
-        for g in range(PASSES):
-            for m in range(TILES):
-                h_bf[g, m] = keep.tile([P, P * PACK], BF16, name="h_bf%d%d" % (g, m), align_bytes=64)
-                h_words[g, m] = keep.tile([P, P], U32, name="h_words%d%d" % (g, m), align_bytes=64)
-                h_scales[g, m] = keep.tile([P, P], U8, name="h_scales%d%d" % (g, m), align_bytes=64)
-
-        def weave(g, m, on_vector):
-            dst = h_bf[g, m][:].rearrange("p (c i t) -> p c t i", i=4, t=PACK)
-            src = h_raw[g][:, :, P * m : P * (m + 1)].rearrange("p t (c i) -> p c t i", i=4)
-            if on_vector:
-                nc.vector.tensor_copy(dst, src)
-            else:
-                nc.scalar.activation(dst, src, ACT.Copy)
-
         scores = [psum.tile([P, S], F32, name="scores%d" % m) for m in range(TILES)]
 
-        def quantise_and_multiply(g, m):
-            nc.vector.quantize_mx(out=h_words[g, m][:].bitcast(FP8X4), scales=h_scales[g, m][:], in_=h_bf[g, m][:])
-            nc.tensor.matmul_mx(
-                out=scores[m][:],
-                lhsT=h_words[g, m][:].bitcast(FP8X4),
-                lhsT_scale=h_scales[g, m][:],
-                rhs=key_words[g][:].bitcast(FP8X4),
-                rhs_scale=key_scales[4 * g : P, :],
-                start=(g == 0),
-                stop=(g == PASSES - 1),
+        def quantise(g, first, count):
+            width = P * count
+            name = "%d%d" % (g, first)
+            h_bf = keep.tile([P, width * PACK], BF16, name="h_bf" + name, tag="stage%d" % (1 + g + first), align_bytes=64)
+            h_words = keep.tile([P, width], U32, name="h_words" + name, align_bytes=64)
+            h_scales = keep.tile([P, width], U8, name="h_scales" + name, align_bytes=64)
+            nc.scalar.activation(
+                h_bf[:].rearrange("p (c i t) -> p c t i", i=4, t=PACK),
+                h_raw[g][:, :, P * first : P * first + width].rearrange("p t (c i) -> p c t i", i=4),
+                ACT.Copy,
             )
+            nc.vector.quantize_mx(out=h_words[:].bitcast(FP8X4), scales=h_scales[:], in_=h_bf[:])
+            for j in range(count):
+                nc.tensor.matmul_mx(
+                    out=scores[first + j][:],
+                    lhsT=h_words[:, P * j : P * (j + 1)].bitcast(FP8X4),
+                    lhsT_scale=h_scales[:, P * j : P * (j + 1)],
+                    rhs=key_words[g][:].bitcast(FP8X4),
+                    rhs_scale=key_scales[4 * g : P, :],
+                    start=(g == 0),
+                    stop=(g == PASSES - 1),
+                )
 
-        weave(0, 0, False)
-        weave(0, 1, True)
-        quantise_and_multiply(0, 0)
-        quantise_and_multiply(0, 1)
+        quantise(0, 0, TILES)
         gather_words(1)
-        weave(1, 0, False)
-        weave(1, 1, True)
-        quantise_and_multiply(1, 0)
-        quantise_and_multiply(1, 1)
+        for m in range(TILES):
+            quantise(1, m, 1)
 
         def small(name, cols=1):
             return [keep.tile([P, cols], F32, name="%s%d" % (name, m)) for m in range(TILES)]
@@ -118,22 +116,34 @@ def tile_picked_ysnapv_avg_p_kernel(tc, x_words, x_scales, hT, offs, out):
         def wide(name):
             return [keep.tile([P, S], F32, name="%s%d" % (name, m), align_bytes=64) for m in range(TILES)]
 
-        neg_max, total, inv, ends, coef, shift = small("neg_max"), small("total"), small("inv"), small("ends"), small("coef", 4), small("shift")
-        sides, three, half_pr, th, gated, result = wide("sides"), wide("three"), wide("half_pr"), wide("th"), wide("gated"), wide("result")
+        neg_max, total, inv, ends, coef, shift = small("neg_max"), small("total"), small("inv"), small("ends", 2), small("coef", 4), small("shift")
+        half_pr, th, gated, result = wide("half_pr"), wide("th"), wide("gated"), wide("result")
+        pairs = [keep.tile([P, HALF + 1], F32, name="pairs%d" % m, align_bytes=64) for m in range(TILES)]
+        three_wide = [keep.tile([P, S + 2 * LEAD], F32, name="three%d" % m, align_bytes=64) for m in range(TILES)]
+        three = [three_wide[m][:, LEAD : LEAD + S] for m in range(TILES)]
+        ex_rows = [ex[m][:, EVEN : EVEN + 2 * ROW].rearrange("p (c i) -> p c i", c=2)[:, :, 0:HALF] for m in range(TILES)]
+        halves = [slice(0, S // 2), slice(S // 2, S)]
 
         for m in range(TILES):
             nc.vector.tensor_reduce(neg_max[m][:], scores[m][:], AX.X, ALU.max, negate=True)
-            nc.scalar.activation(ex[m][:, PAD : PAD + S], scores[m][:], ACT.Exp, bias=neg_max[m][:], accum_out=total[m][:])
+            nc.scalar.activation(ex_rows[m], scores[m][:].rearrange("p (i c) -> p c i", c=2), ACT.Exp, bias=neg_max[m][:], accum_out=total[m][:])
         for m in range(TILES):
+            nc.vector.tensor_tensor(pairs[m][:], ex[m][:, ODD - 1 : ODD + HALF], ex[m][:, EVEN : EVEN + HALF + 1], ALU.add)
             nc.vector.reciprocal(inv[m][:], total[m][:])
-            nc.vector.tensor_tensor(sides[m][:], ex[m][:, PAD - 1 : PAD - 1 + S], ex[m][:, PAD + 1 : PAD + 1 + S], ALU.add)
-            nc.vector.tensor_tensor(three[m][:], sides[m][:], ex[m][:, PAD : PAD + S], ALU.add)
-            nc.scalar.activation(ends[m][:], ex[m][:, PAD : PAD + 1], ACT.Identity, bias=ex[m][:, PAD + S - 1 : PAD + S])
+            nc.vector.tensor_tensor(
+                three_wide[m][:, LEAD - 1 : LEAD + S + 1].rearrange("p (i c) -> p i c", c=2),
+                ex[m][:, EVEN - 1 : EVEN + 1 + 2 * ROW].rearrange("p (c i) -> p i c", c=2)[:, 0 : HALF + 1, :],
+                pairs[m][:].unsqueeze(2).to_broadcast([P, HALF + 1, 2]),
+                ALU.add,
+            )
             nc.scalar.activation(coef[m][:], factors[:], ACT.Copy, scale=inv[m][:])
-            nc.scalar.activation(shift[m][:], ends[m][:], ACT.Copy, scale=coef[m][:, 3:4], bias=-300.0 / S)
-            nc.scalar.activation(half_pr[m][:], ex[m][:, PAD : PAD + S], ACT.Copy, scale=coef[m][:, 1:2])
-            nc.scalar.activation(th[m][:], three[m][:], ACT.Tanh, scale=coef[m][:, 0:1], bias=shift[m][:])
+            nc.scalar.activation(ends[m][:], ex[m][:, EVEN : ODD + HALF : ROW + HALF - 1], ACT.Copy, scale=coef[m][:, 3:4], bias=-150.0 / S, accum_out=shift[m][:])
+            nc.scalar.activation(half_pr[m][:].rearrange("p (i c) -> p i c", c=2), ex_rows[m].rearrange("p c i -> p i c"), ACT.Copy, scale=coef[m][:, 1:2])
+            for h in (halves if m == TILES - 1 else [slice(0, S)]):
+                nc.scalar.activation(th[m][:, h], three[m][:, h], ACT.Tanh, scale=coef[m][:, 0:1], bias=shift[m][:])
         for m in range(TILES):
-            nc.vector.scalar_tensor_tensor(gated[m][:], th[m][:], 1.0, half_pr[m][:], ALU.add, ALU.mult)
-            nc.vector.scalar_tensor_tensor(result[m][:], three[m][:], coef[m][:, 2:3], gated[m][:], ALU.mult, ALU.add)
-            nc.sync.dma_start(out[P * m : P * (m + 1), :], result[m][:])
+            for h in halves:
+                nc.vector.scalar_tensor_tensor(gated[m][:, h], th[m][:, h], 1.0, half_pr[m][:, h], ALU.add, ALU.mult)
+            for h in halves:
+                nc.vector.scalar_tensor_tensor(result[m][:, h], three[m][:, h], coef[m][:, 2:3], gated[m][:, h], ALU.mult, ALU.add)
+                nc.sync.dma_start(out[P * m : P * (m + 1), h], result[m][:, h])

@@ -39,7 +39,7 @@ def tile_picked_ysnapv_avg_p_kernel(tc, x_words, x_scales, hT, offs, out):
         scale_table = keep.tile([P, T], U8, name="scale_table", align_bytes=64)
         nc.gpsimd.memset(scale_table[:].bitcast(I32), 0)
         word_table = [keep.tile([P, T], I32, name="word_table%d" % g, align_bytes=64) for g in range(PASSES)]
-        h_raw = [keep.tile([P, PACK, V], F32, name="h_raw%d" % g, align_bytes=64) for g in range(PASSES)]
+        h_raw = [keep.tile([P, PACK, V], F32, name="h_raw%d" % g, tag="raw%d" % g, align_bytes=64) for g in range(PASSES)]
 
         def load_words(g):
             nc.sync.dma_start(word_table[g][:], x_words[g].rearrange("p n t -> p (n t)").bitcast(I32))
@@ -74,7 +74,7 @@ def tile_picked_ysnapv_avg_p_kernel(tc, x_words, x_scales, hT, offs, out):
         key_words = {}
 
         def gather_words(g):
-            key_words[g] = keep.tile([P, S], U32, name="key_words%d" % g, tag="stage%d" % g, align_bytes=64)
+            key_words[g] = keep.tile([P, S], U32, name="key_words%d" % g, tag="raw%d" % (g - 1), align_bytes=64)
             nc.vector.tensor_copy(key_words[g][:], word_table[g][:].bitcast(U32).indirect(offsets[:]))
 
         gather_words(0)
@@ -85,7 +85,7 @@ def tile_picked_ysnapv_avg_p_kernel(tc, x_words, x_scales, hT, offs, out):
         def quantise(g, first, count):
             width = P * count
             name = "%d%d" % (g, first)
-            h_bf = keep.tile([P, width * PACK], BF16, name="h_bf" + name, tag="stage%d" % (1 + g + first), align_bytes=64)
+            h_bf = keep.tile([P, width * PACK], BF16, name="h_bf" + name, align_bytes=64)
             h_words = keep.tile([P, width], U32, name="h_words" + name, align_bytes=64)
             h_scales = keep.tile([P, width], U8, name="h_scales" + name, align_bytes=64)
             nc.scalar.activation(
@@ -128,18 +128,21 @@ def tile_picked_ysnapv_avg_p_kernel(tc, x_words, x_scales, hT, offs, out):
             nc.vector.tensor_reduce(neg_max[m][:], scores[m][:], AX.X, ALU.max, negate=True)
             nc.scalar.activation(ex_rows[m], scores[m][:].rearrange("p (i c) -> p c i", c=2), ACT.Exp, bias=neg_max[m][:], accum_out=total[m][:])
         for m in range(TILES):
-            nc.vector.tensor_tensor(pairs[m][:], ex[m][:, ODD - 1 : ODD + HALF], ex[m][:, EVEN : EVEN + HALF + 1], ALU.add)
             nc.vector.reciprocal(inv[m][:], total[m][:])
-            nc.vector.tensor_tensor(
-                three_wide[m][:, LEAD - 1 : LEAD + S + 1].rearrange("p (i c) -> p i c", c=2),
-                ex[m][:, EVEN - 1 : EVEN + 1 + 2 * ROW].rearrange("p (c i) -> p i c", c=2)[:, 0 : HALF + 1, :],
-                pairs[m][:].unsqueeze(2).to_broadcast([P, HALF + 1, 2]),
-                ALU.add,
-            )
-            nc.scalar.activation(coef[m][:], factors[:], ACT.Copy, scale=inv[m][:])
+            runs = [slice(0, HALF // 2 + 1), slice(HALF // 2 + 1, HALF + 1)]
+            for r in runs:
+                nc.vector.tensor_tensor(pairs[m][:, r], ex[m][:, ODD - 1 : ODD + HALF][:, r], ex[m][:, EVEN : EVEN + HALF + 1][:, r], ALU.add)
+            nc.vector.tensor_scalar(coef[m][:], factors[:], inv[m][:], None, ALU.mult)
+            for r in runs:
+                nc.vector.tensor_tensor(
+                    three_wide[m][:, LEAD - 1 : LEAD + S + 1].rearrange("p (i c) -> p i c", c=2)[:, r, :],
+                    ex[m][:, EVEN - 1 : EVEN + 1 + 2 * ROW].rearrange("p (c i) -> p i c", c=2)[:, r, :],
+                    pairs[m][:, r].unsqueeze(2).to_broadcast([P, r.stop - r.start, 2]),
+                    ALU.add,
+                )
             nc.scalar.activation(ends[m][:], ex[m][:, EVEN : ODD + HALF : ROW + HALF - 1], ACT.Copy, scale=coef[m][:, 3:4], bias=-150.0 / S, accum_out=shift[m][:])
             nc.scalar.activation(half_pr[m][:].rearrange("p (i c) -> p i c", c=2), ex_rows[m].rearrange("p c i -> p i c"), ACT.Copy, scale=coef[m][:, 1:2])
-            for h in (halves if m == TILES - 1 else [slice(0, S)]):
+            for h in halves:
                 nc.scalar.activation(th[m][:, h], three[m][:, h], ACT.Tanh, scale=coef[m][:, 0:1], bias=shift[m][:])
         for m in range(TILES):
             for h in halves:

@@ -39,13 +39,16 @@ def tile_picked_ysnapv_avg_p_kernel(tc, x_words, x_scales, hT, offs, out):
         scale_table = keep.tile([P, T], U8, name="scale_table", align_bytes=64)
         nc.gpsimd.memset(scale_table[:].bitcast(I32), 0)
         word_table = [keep.tile([P, T], I32, name="word_table%d" % g, align_bytes=64) for g in range(PASSES)]
-        h_raw = [keep.tile([P, PACK, V], F32, name="h_raw%d" % g, tag="raw%d" % g, align_bytes=64) for g in range(PASSES)]
+        h_raw = {}
 
         def load_words(g):
             nc.sync.dma_start(word_table[g][:], x_words[g].rearrange("p n t -> p (n t)").bitcast(I32))
 
-        def load_h(g):
-            nc.sync.dma_start(h_raw[g][:], hT[512 * g : 512 * (g + 1), :].rearrange("(p j) v -> p j v", j=PACK))
+        def load_h(g, first, count):
+            raw = keep.tile([P, PACK, P * count], F32, name="h_raw%d%d" % (g, first), tag="raw%d%d" % (g, first), align_bytes=64)
+            nc.sync.dma_start(raw[:], hT[512 * g : 512 * (g + 1), P * first : P * (first + count)].rearrange("(p j) v -> p j v", j=PACK))
+            for j in range(count):
+                h_raw[g, first + j] = raw[:, :, P * j : P * (j + 1)]
 
         load_words(0)
         nc.sync.dma_start(offsets[:], offs)
@@ -54,9 +57,10 @@ def tile_picked_ysnapv_avg_p_kernel(tc, x_words, x_scales, hT, offs, out):
                 scale_table[32 * q : 32 * q + 4 * PASSES, :].bitcast(I32),
                 x_scales[:, 4 * q : 4 * q + 4, :].bitcast(I32),
             )
-        load_h(0)
+        load_h(0, 0, TILES)
         load_words(1)
-        load_h(1)
+        for m in range(TILES):
+            load_h(1, m, 1)
 
         zero = keep.tile([P, 2, 2], F32, name="zero")
         nc.gpsimd.memset(zero[:], 0.0)
@@ -74,7 +78,7 @@ def tile_picked_ysnapv_avg_p_kernel(tc, x_words, x_scales, hT, offs, out):
         key_words = {}
 
         def gather_words(g):
-            key_words[g] = keep.tile([P, S], U32, name="key_words%d" % g, tag="raw%d" % (g - 1), align_bytes=64)
+            key_words[g] = keep.tile([P, S], U32, name="key_words%d" % g, tag=("key_words0", "raw00")[g], align_bytes=64)
             nc.vector.tensor_copy(key_words[g][:], word_table[g][:].bitcast(U32).indirect(offsets[:]))
 
         gather_words(0)
@@ -82,33 +86,33 @@ def tile_picked_ysnapv_avg_p_kernel(tc, x_words, x_scales, hT, offs, out):
 
         scores = [psum.tile([P, S], F32, name="scores%d" % m) for m in range(TILES)]
 
-        def quantise(g, first, count):
-            width = P * count
-            name = "%d%d" % (g, first)
-            h_bf = keep.tile([P, width * PACK], BF16, name="h_bf" + name, align_bytes=64)
-            h_words = keep.tile([P, width], U32, name="h_words" + name, align_bytes=64)
-            h_scales = keep.tile([P, width], U8, name="h_scales" + name, align_bytes=64)
-            nc.scalar.activation(
-                h_bf[:].rearrange("p (c i t) -> p c t i", i=4, t=PACK),
-                h_raw[g][:, :, P * first : P * first + width].rearrange("p t (c i) -> p c t i", i=4),
-                ACT.Copy,
-            )
+        def quantise(g, m, on_vector):
+            name = "%d%d" % (g, m)
+            h_bf = keep.tile([P, P * PACK], BF16, name="h_bf" + name, align_bytes=64)
+            h_words = keep.tile([P, P], U32, name="h_words" + name, align_bytes=64)
+            h_scales = keep.tile([P, P], U8, name="h_scales" + name, align_bytes=64)
+            dst = h_bf[:].rearrange("p (c i t) -> p c t i", i=4, t=PACK)
+            src = h_raw[g, m].rearrange("p t (c i) -> p c t i", i=4)
+            if on_vector:
+                nc.vector.tensor_copy(dst, src)
+            else:
+                nc.scalar.activation(dst, src, ACT.Copy)
             nc.vector.quantize_mx(out=h_words[:].bitcast(FP8X4), scales=h_scales[:], in_=h_bf[:])
-            for j in range(count):
-                nc.tensor.matmul_mx(
-                    out=scores[first + j][:],
-                    lhsT=h_words[:, P * j : P * (j + 1)].bitcast(FP8X4),
-                    lhsT_scale=h_scales[:, P * j : P * (j + 1)],
-                    rhs=key_words[g][:].bitcast(FP8X4),
-                    rhs_scale=key_scales[4 * g : P, :],
-                    start=(g == 0),
-                    stop=(g == PASSES - 1),
-                )
+            nc.tensor.matmul_mx(
+                out=scores[m][:],
+                lhsT=h_words[:].bitcast(FP8X4),
+                lhsT_scale=h_scales[:],
+                rhs=key_words[g][:].bitcast(FP8X4),
+                rhs_scale=key_scales[4 * g : P, :],
+                start=(g == 0),
+                stop=(g == PASSES - 1),
+            )
 
-        quantise(0, 0, TILES)
+        quantise(0, 0, False)
+        quantise(0, 1, True)
         gather_words(1)
         for m in range(TILES):
-            quantise(1, m, 1)
+            quantise(1, m, False)
 
         def small(name, cols=1):
             return [keep.tile([P, cols], F32, name="%s%d" % (name, m)) for m in range(TILES)]

from contextlib import ExitStack

import concourse.mybir as mybir

K, T, S, V = 1024, 1024, 512, 256
FLOPS = 2 * K * S * V

F32 = mybir.dt.float32
BF16 = mybir.dt.bfloat16
I32 = mybir.dt.int32
U32 = mybir.dt.uint32
U16 = mybir.dt.uint16
U8 = mybir.dt.uint8
FP8X4 = mybir.dt.float8_e4m3fn_x4
ALU = mybir.AluOpType
ACT = mybir.ActivationFunctionType
AX = mybir.AxisListType

P = 128
PACK = 4
PASSES = K // (P * PACK)
TILES = V // P
HALF = S // 2
EVEN = 4
ROW = HALF + 4
ODD = EVEN + ROW
EX_COLS = 528
LEAD = 4


def tile_picked_ysnapv_avg_p_kernel(tc, x_words, x_scales, hT, offs, out):
    nc = tc.nc
    with ExitStack() as ctx:
        keep = ctx.enter_context(tc.tile_pool(name="keep", bufs=1))
        psum = ctx.enter_context(tc.psum_pool(name="psum", bufs=1))

        offsets = keep.tile([P, S // 16], U16, name="offsets")

        scale_table = keep.tile([P, T], U8, name="scale_table", align_bytes=64)
        nc.gpsimd.memset(scale_table[:].bitcast(I32), 0)
        word_table = [keep.tile([P, T], I32, name="word_table%d" % g, align_bytes=64) for g in range(PASSES)]
        h_raw = {}

        def load_words(g):
            nc.sync.dma_start(word_table[g][:], x_words[g].rearrange("p n t -> p (n t)").bitcast(I32))

        def load_h(g, first, count):
            raw = keep.tile([P, PACK, P * count], F32, name="h_raw%d%d" % (g, first), tag="raw%d%d" % (g, first), align_bytes=64)
            nc.sync.dma_start(raw[:], hT[512 * g : 512 * (g + 1), P * first : P * (first + count)].rearrange("(p j) v -> p j v", j=PACK))
            for j in range(count):
                h_raw[g, first + j] = raw[:, :, P * j : P * (j + 1)]

        load_words(0)
        nc.sync.dma_start(offsets[:], offs)
        for q in range(4):
            nc.sync.dma_start(
                scale_table[32 * q : 32 * q + 4 * PASSES, :].bitcast(I32),
                x_scales[:, 4 * q : 4 * q + 4, :].bitcast(I32),
            )
        load_h(0, 0, TILES)
        load_words(1)
        for m in range(TILES):
            load_h(1, m, 1)

        zero = keep.tile([P, 2, 2], F32, name="zero")
        nc.gpsimd.memset(zero[:], 0.0)
        ex = [keep.tile([P, EX_COLS], F32, name="ex%d" % m, align_bytes=64) for m in range(TILES)]
        for m in range(TILES):
            borders = ex[m][:, EVEN - 1 : EVEN - 1 + 2 * ROW].rearrange("p (c i) -> p c i", c=2)[:, :, 0 : HALF + 2 : HALF + 1]
            nc.scalar.activation(borders, zero[:], ACT.Copy)
        numer = keep.tile([P, 4], F32, name="numer")
        for col, value in enumerate((200.0, 150.0, 20.0, 300.0 / S)):
            nc.gpsimd.memset(numer[:, col : col + 1], value)
        factors = keep.tile([P, 4], F32, name="factors")
        nc.gpsimd.tensor_scalar(factors[:], numer[:], 1.0 / 3.0, 0.0, ALU.mult, ALU.add)

        key_scales = keep.tile([P, S], U8, name="key_scales", align_bytes=64)
        key_words = {}

        def gather_words(g):
            key_words[g] = keep.tile([P, S], U32, name="key_words%d" % g, tag=("key_words0", "raw00")[g], align_bytes=64)
            nc.vector.tensor_copy(key_words[g][:], word_table[g][:].bitcast(U32).indirect(offsets[:]))

        gather_words(0)
        nc.vector.tensor_copy(key_scales[:], scale_table[:].indirect(offsets[:]))

        scores = [psum.tile([P, S], F32, name="scores%d" % m) for m in range(TILES)]

        def quantise(g, m, on_vector):
            name = "%d%d" % (g, m)
            h_bf = keep.tile([P, P * PACK], BF16, name="h_bf" + name, align_bytes=64)
            h_words = keep.tile([P, P], U32, name="h_words" + name, align_bytes=64)
            h_scales = keep.tile([P, P], U8, name="h_scales" + name, align_bytes=64)
            dst = h_bf[:].rearrange("p (c i t) -> p c t i", i=4, t=PACK)
            src = h_raw[g, m].rearrange("p t (c i) -> p c t i", i=4)
            if on_vector:
                nc.vector.tensor_copy(dst, src)
            else:
                nc.scalar.activation(dst, src, ACT.Copy)
            nc.vector.quantize_mx(out=h_words[:].bitcast(FP8X4), scales=h_scales[:], in_=h_bf[:])
            nc.tensor.matmul_mx(
                out=scores[m][:],
                lhsT=h_words[:].bitcast(FP8X4),
                lhsT_scale=h_scales[:],
                rhs=key_words[g][:].bitcast(FP8X4),
                rhs_scale=key_scales[4 * g : P, :],
                start=(g == 0),
                stop=(g == PASSES - 1),
            )

        quantise(0, 0, False)
        quantise(0, 1, True)
        gather_words(1)
        for m in range(TILES):
            quantise(1, m, False)

        def small(name, cols=1):
            return [keep.tile([P, cols], F32, name="%s%d" % (name, m)) for m in range(TILES)]

        def wide(name):
            return [keep.tile([P, S], F32, name="%s%d" % (name, m), align_bytes=64) for m in range(TILES)]

        neg_max, total, inv, ends, coef, shift = small("neg_max"), small("total"), small("inv"), small("ends", 2), small("coef", 4), small("shift")
        half_pr, th, gated, result = wide("half_pr"), wide("th"), wide("gated"), wide("result")
        pairs = [keep.tile([P, HALF + 1], F32, name="pairs%d" % m, align_bytes=64) for m in range(TILES)]
        three_wide = [keep.tile([P, S + 2 * LEAD], F32, name="three%d" % m, align_bytes=64) for m in range(TILES)]
        three = [three_wide[m][:, LEAD : LEAD + S] for m in range(TILES)]
        ex_rows = [ex[m][:, EVEN : EVEN + 2 * ROW].rearrange("p (c i) -> p c i", c=2)[:, :, 0:HALF] for m in range(TILES)]
        halves = [slice(0, S // 2), slice(S // 2, S)]

        for m in range(TILES):
            nc.vector.tensor_reduce(neg_max[m][:], scores[m][:], AX.X, ALU.max, negate=True)
            nc.scalar.activation(ex_rows[m], scores[m][:].rearrange("p (i c) -> p c i", c=2), ACT.Exp, bias=neg_max[m][:], accum_out=total[m][:])
        for m in range(TILES):
            nc.vector.reciprocal(inv[m][:], total[m][:])
            runs = [slice(0, HALF // 2 + 1), slice(HALF // 2 + 1, HALF + 1)]
            for r in runs:
                nc.vector.tensor_tensor(pairs[m][:, r], ex[m][:, ODD - 1 : ODD + HALF][:, r], ex[m][:, EVEN : EVEN + HALF + 1][:, r], ALU.add)
            nc.vector.tensor_scalar(coef[m][:], factors[:], inv[m][:], None, ALU.mult)
            for r in runs:
                nc.vector.tensor_tensor(
                    three_wide[m][:, LEAD - 1 : LEAD + S + 1].rearrange("p (i c) -> p i c", c=2)[:, r, :],
                    ex[m][:, EVEN - 1 : EVEN + 1 + 2 * ROW].rearrange("p (c i) -> p i c", c=2)[:, r, :],
                    pairs[m][:, r].unsqueeze(2).to_broadcast([P, r.stop - r.start, 2]),
                    ALU.add,
                )
            nc.scalar.activation(ends[m][:], ex[m][:, EVEN : ODD + HALF : ROW + HALF - 1], ACT.Copy, scale=coef[m][:, 3:4], bias=-150.0 / S, accum_out=shift[m][:])
            nc.scalar.activation(half_pr[m][:].rearrange("p (i c) -> p i c", c=2), ex_rows[m].rearrange("p c i -> p i c"), ACT.Copy, scale=coef[m][:, 1:2])
            for h in halves:
                nc.scalar.activation(th[m][:, h], three[m][:, h], ACT.Tanh, scale=coef[m][:, 0:1], bias=shift[m][:])
        for m in range(TILES):
            for h in halves:
                nc.vector.scalar_tensor_tensor(gated[m][:, h], th[m][:, h], 1.0, half_pr[m][:, h], ALU.add, ALU.mult)
            for h in halves:
                nc.vector.scalar_tensor_tensor(result[m][:, h], three[m][:, h], coef[m][:, 2:3], gated[m][:, h], ALU.mult, ALU.add)
                nc.sync.dma_start(out[P * m : P * (m + 1), h], result[m][:, h])
